import numpy as np
import ml_dtypes


def mxq(x, axis, fmt="e4m3"):
    dtype, down = {"e4m3": (ml_dtypes.float8_e4m3fn, 7), "e5m2": (ml_dtypes.float8_e5m2, 14)}[fmt]
    v = np.moveaxis(np.asarray(x, np.float32).astype(ml_dtypes.bfloat16).astype(np.float64), axis, -1)
    blocks = v.reshape(v.shape[:-1] + (-1, 32))
    amax = np.abs(blocks).max(-1, keepdims=True)
    byte = np.maximum(np.where(amax > 0, np.frexp(amax)[1] - 1 + 127, 0) - down, 1)
    scale = np.exp2(byte - 127.0)
    codes = (blocks / scale).astype(np.float32).astype(dtype).astype(np.float64)
    return np.moveaxis((codes * scale).reshape(v.shape), -1, axis)


WIDE = False


def mx_kscale(k):
    if not WIDE:
        return np.ones(k)
    levels = np.array([10, -10, 5, -5, 0])
    if k % 512:
        return np.exp2(np.random.permutation(np.resize(levels, k // 32))).repeat(32)
    a = np.empty((k // 512, 16))
    for p in range(k // 512):
        a[p, :8] = np.random.permutation(np.resize(levels, 8))
        for g in range(8):
            far = levels[np.abs(levels - a[p, g]) >= 10]
            a[p, g + 8] = far[np.random.randint(len(far))]
    return np.exp2(a.ravel()).repeat(32)


def f64(x):
    return np.asarray(x).astype(np.float64)


def striped(idx):
    return np.tile(idx.reshape(-1, 16).T, (8, 1)).astype(np.uint16)


def unstriped(offs):
    return offs[:16].T.reshape(-1).astype(np.int64)


def pack_weight(w):
    k, n = w.shape
    w = f64(np.asarray(w, np.float32).astype(ml_dtypes.bfloat16)).reshape(k // 32, 32, n)
    amax = np.abs(w).max(1)
    byte = np.clip(np.where(amax > 0, np.frexp(amax)[1] - 1 + 127 - 7, 1), 1, 254)
    scaled = (w * np.exp2(127.0 - byte)[:, None, :]).reshape(k, n).astype(np.float32)
    words = np.ascontiguousarray(scaled.reshape(k // 512, 128, 4, n).transpose(0, 1, 3, 2)).astype(ml_dtypes.float8_e4m3fn).view(np.uint8)
    return words, np.ascontiguousarray(byte.astype(np.uint8).reshape(k // 512, 16, n))


def unpack_weight(words, scales):
    g, p, n, _ = words.shape
    vals = np.ascontiguousarray(words).view(ml_dtypes.float8_e4m3fn).astype(np.float64) * np.repeat(np.exp2(scales.astype(np.float64) - 127.0), 8, axis=1)[..., None]
    return vals.transpose(0, 1, 3, 2).reshape(g * 512, n)


def relu(v):
    return np.maximum(v, 0.0)


def sigmoid(v):
    return 1.0 / (1.0 + np.exp(-np.maximum(v, -700.0)))


K, T, S, V, H = 512, 2048, 512, 512, 512


def setup_inputs():
    n = np.random.standard_normal
    s = mx_kscale(K)[:, None]
    packed_xT = pack_weight(n((K, T)) * s)
    return {
        "x_words": packed_xT[0],
        "x_scales": packed_xT[1],
        "w1": (n((K, H)) / np.sqrt(K) / s).astype(np.float32),
        "gs": (np.random.uniform(0.5, 1.5, (K, 1)) / s).astype(np.float32),
        "offs": striped(np.random.permutation(T)[:S]),
        "ca": striped(np.random.permutation(T)[:V]),
        "cb": striped(np.random.permutation(T)[:V]),
    }


def reference(x_words, x_scales, w1, gs, offs, ca, cb):
    x_ca = unpack_weight(x_words, x_scales)[:, unstriped(ca)]
    xq = unpack_weight(x_words, x_scales)[:, unstriped(offs)]
    h = relu(mxq(f64(w1), 0, "e4m3").T @ xq)
    z = f64(gs) * h
    zq = mxq(z, 0, "e4m3")
    a = 0.0625 * (x_ca.T @ zq)
    x_cb = unpack_weight(x_words, x_scales)[:, unstriped(cb)]
    b = 0.0625 * (x_cb.T @ zq)
    return sigmoid(a - b)

@@ -1,0 +1,132 @@
+from contextlib import ExitStack
+
+import concourse.mybir as mybir
+
+K, T, S, V, H = 512, 2048, 512, 512, 512
+FLOPS = 2 * K * H * S + 2 * 2 * H * V * S
+
+F32 = mybir.dt.float32
+BF16 = mybir.dt.bfloat16
+I32 = mybir.dt.int32
+U32 = mybir.dt.uint32
+U16 = mybir.dt.uint16
+U8 = mybir.dt.uint8
+FP8X4 = mybir.dt.float8_e4m3fn_x4
+ALU = mybir.AluOpType
+ACT = mybir.ActivationFunctionType
+
+P = 128
+PACK = 4
+CHUNK = 128
+W_PIECES = 2
+
+
+def tile_picked_candtwo_sigmoid_p_kernel(tc, x_words, x_scales, w1, gs, offs, ca, cb, out):
+    nc = tc.nc
+    with ExitStack() as ctx:
+        keep = ctx.enter_context(tc.tile_pool(name="keep", bufs=1))
+        shared = ctx.enter_context(tc.tile_pool(name="shared", bufs=1))
+        psum = ctx.enter_context(tc.psum_pool(name="psum", bufs=1))
+
+        offs_t = keep.tile([P, S // 16], U16, name="offs_t")
+        ca_t = keep.tile([P, V // 16], U16, name="ca_t")
+        cb_t = keep.tile([P, V // 16], U16, name="cb_t")
+        words = keep.tile([P, T], U32, name="words", align_bytes=64)
+        scales = shared.tile([P, T], U8, name="scales", align_bytes=64, offset=T // 2)
+        gs_t = keep.tile([P, PACK], F32, name="gs_t")
+
+        nc.vector.memset(scales[:].bitcast(I32), 0)
+        nc.sync.dma_start(offs_t[:], offs)
+        for q in range(4):
+            nc.scalar.dma_start(scales[32 * q : 32 * q + 4, :].bitcast(I32), x_scales[0, 4 * q : 4 * q + 4, :].bitcast(I32))
+        nc.sync.dma_start(ca_t[:], ca)
+        nc.sync.dma_start(cb_t[:], cb)
+        nc.sync.dma_start(words[:].bitcast(I32), x_words[0].rearrange("p n t -> p (n t)").bitcast(I32))
+        w_rows = w1.rearrange("(p j) c -> p j c", j=PACK)
+        wc = H // W_PIECES
+        w_raw = []
+        for i in range(W_PIECES):
+            raw = keep.tile([P, PACK, wc], F32, name="w_raw%d" % i)
+            nc.sync.dma_start(raw[:], w_rows[:, :, i * wc : (i + 1) * wc])
+            w_raw.append(raw)
+        nc.sync.dma_start(gs_t[:], gs.rearrange("(p t) o -> p (t o)", t=PACK))
+
+        def gather(name, table, dtype, lst, tag=None, offset=None):
+            if offset is None:
+                g = keep.tile([P, S], dtype, name=name, tag=tag or name, align_bytes=64)
+            else:
+                g = shared.tile([P, S], dtype, name=name, align_bytes=64, offset=offset)
+            nc.vector.tensor_copy(g[:], table[:].indirect(lst[:]))
+            return g
+
+        xs_s = gather("xs_s", scales, U8, offs_t)
+        xa_s = gather("xa_s", scales, U8, ca_t)
+        xb_s = gather("xb_s", scales, U8, cb_t)
+        xs_w = gather("xs_w", words, U32, offs_t, offset=0)
+        xa_w = gather("xa_w", words, U32, ca_t, offset=T)
+
+        w_bf = keep.tile([P, PACK, P, PACK], BF16, name="w_bf", tag="w_bf", align_bytes=64)
+        mc = wc // PACK
+        for i in range(W_PIECES):
+            nc.scalar.copy(
+                w_bf[:, :, i * mc : (i + 1) * mc, :].rearrange("p t m j -> p m t j"),
+                w_raw[i][:].rearrange("p j (m t) -> p m t j", t=PACK),
+            )
+        w_c = keep.tile([P, H], U32, name="w_c", align_bytes=64)
+        w_s = keep.tile([P, H], U8, name="w_s", align_bytes=64)
+        nc.vector.quantize_mx(out=w_c[:].bitcast(FP8X4), scales=w_s[:], in_=w_bf[:].rearrange("p t m j -> p (t m j)"))
+
+        xb_w = gather("xb_w", words, U32, cb_t, tag="w_bf")
+
+        n_chunks = S // CHUNK
+        h_banks = []
+        for c in range(n_chunks):
+            cols = slice(c * CHUNK, (c + 1) * CHUNK)
+            h = psum.tile([P, PACK, CHUNK], F32, name="h%d" % c)
+            for t in range(PACK):
+                ch = slice(t * P, (t + 1) * P)
+                nc.tensor.matmul_mx(
+                    out=h[:, t, :],
+                    lhsT=w_c[:, ch].bitcast(FP8X4),
+                    lhsT_scale=w_s[:, ch],
+                    rhs=xs_w[:, cols].bitcast(FP8X4),
+                    rhs_scale=xs_s[:, cols],
+                    start=True,
+                    stop=True,
+                )
+            h_banks.append(h)
+
+        out_v = out.rearrange("(v p) s -> p v s", p=P)
+        for c in range(n_chunks):
+            cols = slice(c * CHUNK, (c + 1) * CHUNK)
+            z = keep.tile([P, 2, CHUNK, PACK], BF16, name="z%d" % c, align_bytes=64)
+            nc.vector.scalar_tensor_tensor(
+                out=z[:, 0, :, :],
+                in0=h_banks[c][:].rearrange("p t n -> p n t"),
+                scalar=0.0,
+                in1=gs_t[:].unsqueeze(1).to_broadcast([P, CHUNK, PACK]),
+                op0=ALU.max,
+                op1=ALU.mult,
+            )
+            nc.vector.tensor_scalar(out=z[:, 1, :, :], in0=z[:, 0, :, :], scalar1=-1.0, scalar2=None, op0=ALU.mult)
+            z_c = keep.tile([P, 2 * CHUNK], U32, name="z_c%d" % c, align_bytes=64)
+            z_s = keep.tile([P, 2 * CHUNK], U8, name="z_s%d" % c, align_bytes=64)
+            nc.vector.quantize_mx(out=z_c[:].bitcast(FP8X4), scales=z_s[:], in_=z[:].rearrange("p s n t -> p (s n t)"))
+
+            d = psum.tile([P, V // P, CHUNK], F32, name="d%d" % c)
+            for v in range(V // P):
+                rows = slice(v * P, (v + 1) * P)
+                for s, (xw, xs) in enumerate(((xa_w, xa_s), (xb_w, xb_s))):
+                    zc = slice(s * CHUNK, (s + 1) * CHUNK)
+                    nc.tensor.matmul_mx(
+                        out=d[:, v, :],
+                        lhsT=xw[:, rows].bitcast(FP8X4),
+                        lhsT_scale=xs[:, rows],
+                        rhs=z_c[:, zc].bitcast(FP8X4),
+                        rhs_scale=z_s[:, zc],
+                        start=(s == 0),
+                        stop=(s == 1),
+                    )
+            res = keep.tile([P, V // P, CHUNK], F32, name="res%d" % c)
+            nc.scalar.activation(res[:], d[:], ACT.Sigmoid, scale=0.0625)
+            nc.sync.dma_start(out_v[:, :, cols], res[:])

@@ -18,7 +18,7 @@ ACT = mybir.ActivationFunctionType
 P = 128
 PACK = 4
 CHUNK = 128
-W_PIECES = 2
+W_SPLIT = (0, 384, 512)
 
 
 def tile_picked_candtwo_sigmoid_p_kernel(tc, x_words, x_scales, w1, gs, offs, ca, cb, out):
@@ -32,28 +32,29 @@ def tile_picked_candtwo_sigmoid_p_kernel(tc, x_words, x_scales, w1, gs, offs, ca
         ca_t = keep.tile([P, V // 16], U16, name="ca_t")
         cb_t = keep.tile([P, V // 16], U16, name="cb_t")
         words = keep.tile([P, T], U32, name="words", align_bytes=64)
-        scales = shared.tile([P, T], U8, name="scales", align_bytes=64, offset=T // 2)
+        scales = keep.tile([P, T], U8, name="scales", align_bytes=64)
         gs_t = keep.tile([P, PACK], F32, name="gs_t")
 
         nc.vector.memset(scales[:].bitcast(I32), 0)
         nc.sync.dma_start(offs_t[:], offs)
-        for q in range(4):
-            nc.scalar.dma_start(scales[32 * q : 32 * q + 4, :].bitcast(I32), x_scales[0, 4 * q : 4 * q + 4, :].bitcast(I32))
         nc.sync.dma_start(ca_t[:], ca)
         nc.sync.dma_start(cb_t[:], cb)
-        nc.sync.dma_start(words[:].bitcast(I32), x_words[0].rearrange("p n t -> p (n t)").bitcast(I32))
+        for q in range(4):
+            queue = nc.sync if q < 2 else nc.scalar
+            queue.dma_start(scales[32 * q : 32 * q + 4, :].bitcast(I32), x_scales[0, 4 * q : 4 * q + 4, :].bitcast(I32))
         w_rows = w1.rearrange("(p j) c -> p j c", j=PACK)
-        wc = H // W_PIECES
+        w_pieces = list(zip(W_SPLIT[:-1], W_SPLIT[1:]))
         w_raw = []
-        for i in range(W_PIECES):
-            raw = keep.tile([P, PACK, wc], F32, name="w_raw%d" % i)
-            nc.sync.dma_start(raw[:], w_rows[:, :, i * wc : (i + 1) * wc])
+        for lo, hi in w_pieces:
+            raw = keep.tile([P, PACK, hi - lo], F32, name="w_raw%d" % lo)
+            nc.sync.dma_start(raw[:], w_rows[:, :, lo:hi])
             w_raw.append(raw)
+        nc.sync.dma_start(words[:].bitcast(I32), x_words[0].rearrange("p n t -> p (n t)").bitcast(I32))
         nc.sync.dma_start(gs_t[:], gs.rearrange("(p t) o -> p (t o)", t=PACK))
 
-        def gather(name, table, dtype, lst, tag=None, offset=None):
+        def gather(name, table, dtype, lst, offset=None):
             if offset is None:
-                g = keep.tile([P, S], dtype, name=name, tag=tag or name, align_bytes=64)
+                g = keep.tile([P, S], dtype, name=name, align_bytes=64)
             else:
                 g = shared.tile([P, S], dtype, name=name, align_bytes=64, offset=offset)
             nc.vector.tensor_copy(g[:], table[:].indirect(lst[:]))
@@ -62,21 +63,20 @@ def tile_picked_candtwo_sigmoid_p_kernel(tc, x_words, x_scales, w1, gs, offs, ca
         xs_s = gather("xs_s", scales, U8, offs_t)
         xa_s = gather("xa_s", scales, U8, ca_t)
         xb_s = gather("xb_s", scales, U8, cb_t)
-        xs_w = gather("xs_w", words, U32, offs_t, offset=0)
-        xa_w = gather("xa_w", words, U32, ca_t, offset=T)
 
-        w_bf = keep.tile([P, PACK, P, PACK], BF16, name="w_bf", tag="w_bf", align_bytes=64)
-        mc = wc // PACK
-        for i in range(W_PIECES):
+        w_bf = shared.tile([P, PACK, P, PACK], BF16, name="w_bf", align_bytes=64, offset=1024)
+        for raw, (lo, hi) in zip(w_raw, w_pieces):
             nc.scalar.copy(
-                w_bf[:, :, i * mc : (i + 1) * mc, :].rearrange("p t m j -> p m t j"),
-                w_raw[i][:].rearrange("p j (m t) -> p m t j", t=PACK),
+                w_bf[:, :, lo // PACK : hi // PACK, :].rearrange("p t m j -> p m t j"),
+                raw[:].rearrange("p j (m t) -> p m t j", t=PACK),
             )
         w_c = keep.tile([P, H], U32, name="w_c", align_bytes=64)
         w_s = keep.tile([P, H], U8, name="w_s", align_bytes=64)
         nc.vector.quantize_mx(out=w_c[:].bitcast(FP8X4), scales=w_s[:], in_=w_bf[:].rearrange("p t m j -> p (t m j)"))
 
-        xb_w = gather("xb_w", words, U32, cb_t, tag="w_bf")
+        xs_w = gather("xs_w", words, U32, offs_t, offset=0)
+        xa_w = gather("xa_w", words, U32, ca_t, offset=2048)
+        xb_w = gather("xb_w", words, U32, cb_t, offset=4096)
 
         n_chunks = S // CHUNK
         h_banks = []
@@ -97,7 +97,9 @@ def tile_picked_candtwo_sigmoid_p_kernel(tc, x_words, x_scales, w1, gs, offs, ca
             h_banks.append(h)
 
         out_v = out.rearrange("(v p) s -> p v s", p=P)
+        n_blocks = V // P
         for c in range(n_chunks):
+            last = c == n_chunks - 1
             cols = slice(c * CHUNK, (c + 1) * CHUNK)
             z = keep.tile([P, 2, CHUNK, PACK], BF16, name="z%d" % c, align_bytes=64)
             nc.vector.scalar_tensor_tensor(
@@ -108,25 +110,41 @@ def tile_picked_candtwo_sigmoid_p_kernel(tc, x_words, x_scales, w1, gs, offs, ca
                 op0=ALU.max,
                 op1=ALU.mult,
             )
-            nc.vector.tensor_scalar(out=z[:, 1, :, :], in0=z[:, 0, :, :], scalar1=-1.0, scalar2=None, op0=ALU.mult)
             z_c = keep.tile([P, 2 * CHUNK], U32, name="z_c%d" % c, align_bytes=64)
             z_s = keep.tile([P, 2 * CHUNK], U8, name="z_s%d" % c, align_bytes=64)
-            nc.vector.quantize_mx(out=z_c[:].bitcast(FP8X4), scales=z_s[:], in_=z[:].rearrange("p s n t -> p (s n t)"))
 
-            d = psum.tile([P, V // P, CHUNK], F32, name="d%d" % c)
-            for v in range(V // P):
-                rows = slice(v * P, (v + 1) * P)
-                for s, (xw, xs) in enumerate(((xa_w, xa_s), (xb_w, xb_s))):
-                    zc = slice(s * CHUNK, (s + 1) * CHUNK)
-                    nc.tensor.matmul_mx(
-                        out=d[:, v, :],
-                        lhsT=xw[:, rows].bitcast(FP8X4),
-                        lhsT_scale=xs[:, rows],
-                        rhs=z_c[:, zc].bitcast(FP8X4),
-                        rhs_scale=z_s[:, zc],
-                        start=(s == 0),
-                        stop=(s == 1),
-                    )
-            res = keep.tile([P, V // P, CHUNK], F32, name="res%d" % c)
-            nc.scalar.activation(res[:], d[:], ACT.Sigmoid, scale=0.0625)
-            nc.sync.dma_start(out_v[:, :, cols], res[:])
+            def quantise(s0, s1):
+                zc = slice(s0 * CHUNK, s1 * CHUNK)
+                nc.vector.quantize_mx(out=z_c[:, zc].bitcast(FP8X4), scales=z_s[:, zc], in_=z[:, s0:s1, :, :].rearrange("p s n t -> p (s n t)"))
+
+            if last:
+                quantise(0, 1)
+            nc.vector.tensor_scalar(out=z[:, 1, :, :], in0=z[:, 0, :, :], scalar1=-1.0, scalar2=None, op0=ALU.mult)
+            if last:
+                quantise(1, 2)
+            else:
+                quantise(0, 2)
+
+            groups = [(0, 2), (2, 4)] if last else [(0, 4)]
+            banks = []
+            for g, (v0, v1) in enumerate(groups):
+                tag = "d%d" % c if g == 0 else "h0"
+                banks.append(psum.tile([P, v1 - v0, CHUNK], F32, name="d%d_%d" % (c, g), tag=tag))
+            for s, (xw, xs) in enumerate(((xa_w, xa_s), (xb_w, xb_s))):
+                zc = slice(s * CHUNK, (s + 1) * CHUNK)
+                for d, (v0, v1) in zip(banks, groups):
+                    for v in range(v0, v1):
+                        rows = slice(v * P, (v + 1) * P)
+                        nc.tensor.matmul_mx(
+                            out=d[:, v - v0, :],
+                            lhsT=xw[:, rows].bitcast(FP8X4),
+                            lhsT_scale=xs[:, rows],
+                            rhs=z_c[:, zc].bitcast(FP8X4),
+                            rhs_scale=z_s[:, zc],
+                            start=(s == 0 and v == v0),
+                            stop=(s == 1 and v == v1 - 1),
+                        )
+            for g, (d, (v0, v1)) in enumerate(zip(banks, groups)):
+                res = keep.tile([P, v1 - v0, CHUNK], F32, name="res%d_%d" % (c, g))
+                nc.scalar.activation(res[:], d[:], ACT.Sigmoid, scale=0.0625)
+                nc.sync.dma_start(out_v[:, v0:v1, cols], res[:])

@@ -18,7 +18,7 @@ ACT = mybir.ActivationFunctionType
 P = 128
 PACK = 4
 CHUNK = 128
-W_SPLIT = (0, 384, 512)
+W_SPLIT = (0, 256, 512)
 
 
 def tile_picked_candtwo_sigmoid_p_kernel(tc, x_words, x_scales, w1, gs, offs, ca, cb, out):
@@ -32,7 +32,7 @@ def tile_picked_candtwo_sigmoid_p_kernel(tc, x_words, x_scales, w1, gs, offs, ca
         ca_t = keep.tile([P, V // 16], U16, name="ca_t")
         cb_t = keep.tile([P, V // 16], U16, name="cb_t")
         words = keep.tile([P, T], U32, name="words", align_bytes=64)
-        scales = keep.tile([P, T], U8, name="scales", align_bytes=64)
+        scales = shared.tile([P, T], U8, name="scales", align_bytes=64, offset=1024)
         gs_t = keep.tile([P, PACK], F32, name="gs_t")
 
         nc.vector.memset(scales[:].bitcast(I32), 0)
@@ -42,6 +42,10 @@ def tile_picked_candtwo_sigmoid_p_kernel(tc, x_words, x_scales, w1, gs, offs, ca
         for q in range(4):
             queue = nc.sync if q < 2 else nc.scalar
             queue.dma_start(scales[32 * q : 32 * q + 4, :].bitcast(I32), x_scales[0, 4 * q : 4 * q + 4, :].bitcast(I32))
+        warm = keep.tile([P, 2], F32, name="warm")
+        nc.vector.memset(warm[:, 0:1], 0.0)
+        nc.scalar.activation(warm[:, 1:2], warm[:, 0:1], ACT.Sigmoid, scale=0.0625)
+        nc.sync.dma_start(words[:].bitcast(I32), x_words[0].rearrange("p n t -> p (n t)").bitcast(I32))
         w_rows = w1.rearrange("(p j) c -> p j c", j=PACK)
         w_pieces = list(zip(W_SPLIT[:-1], W_SPLIT[1:]))
         w_raw = []
@@ -49,7 +53,6 @@ def tile_picked_candtwo_sigmoid_p_kernel(tc, x_words, x_scales, w1, gs, offs, ca
             raw = keep.tile([P, PACK, hi - lo], F32, name="w_raw%d" % lo)
             nc.sync.dma_start(raw[:], w_rows[:, :, lo:hi])
             w_raw.append(raw)
-        nc.sync.dma_start(words[:].bitcast(I32), x_words[0].rearrange("p n t -> p (n t)").bitcast(I32))
         nc.sync.dma_start(gs_t[:], gs.rearrange("(p t) o -> p (t o)", t=PACK))
 
         def gather(name, table, dtype, lst, offset=None):
@@ -63,8 +66,10 @@ def tile_picked_candtwo_sigmoid_p_kernel(tc, x_words, x_scales, w1, gs, offs, ca
         xs_s = gather("xs_s", scales, U8, offs_t)
         xa_s = gather("xa_s", scales, U8, ca_t)
         xb_s = gather("xb_s", scales, U8, cb_t)
+        xs_w = gather("xs_w", words, U32, offs_t, offset=0)
+        xa_w = gather("xa_w", words, U32, ca_t, offset=2048)
 
-        w_bf = shared.tile([P, PACK, P, PACK], BF16, name="w_bf", align_bytes=64, offset=1024)
+        w_bf = shared.tile([P, PACK, P, PACK], BF16, name="w_bf", align_bytes=64, offset=4096)
         for raw, (lo, hi) in zip(w_raw, w_pieces):
             nc.scalar.copy(
                 w_bf[:, :, lo // PACK : hi // PACK, :].rearrange("p t m j -> p m t j"),
@@ -74,8 +79,6 @@ def tile_picked_candtwo_sigmoid_p_kernel(tc, x_words, x_scales, w1, gs, offs, ca
         w_s = keep.tile([P, H], U8, name="w_s", align_bytes=64)
         nc.vector.quantize_mx(out=w_c[:].bitcast(FP8X4), scales=w_s[:], in_=w_bf[:].rearrange("p t m j -> p (t m j)"))
 
-        xs_w = gather("xs_w", words, U32, offs_t, offset=0)
-        xa_w = gather("xa_w", words, U32, ca_t, offset=2048)
         xb_w = gather("xb_w", words, U32, cb_t, offset=4096)
 
         n_chunks = S // CHUNK
@@ -98,53 +101,58 @@ def tile_picked_candtwo_sigmoid_p_kernel(tc, x_words, x_scales, w1, gs, offs, ca
 
         out_v = out.rearrange("(v p) s -> p v s", p=P)
         n_blocks = V // P
-        for c in range(n_chunks):
-            last = c == n_chunks - 1
-            cols = slice(c * CHUNK, (c + 1) * CHUNK)
-            z = keep.tile([P, 2, CHUNK, PACK], BF16, name="z%d" % c, align_bytes=64)
+        z = [keep.tile([P, 2, CHUNK, PACK], BF16, name="z%d" % c, align_bytes=64) for c in range(n_chunks)]
+
+        def weigh(c):
             nc.vector.scalar_tensor_tensor(
-                out=z[:, 0, :, :],
+                out=z[c][:, 0, :, :],
                 in0=h_banks[c][:].rearrange("p t n -> p n t"),
                 scalar=0.0,
                 in1=gs_t[:].unsqueeze(1).to_broadcast([P, CHUNK, PACK]),
                 op0=ALU.max,
                 op1=ALU.mult,
             )
+
+        def negate(c):
+            if c in (0, 1, 2):
+                nc.scalar.activation(z[c][:, 1, :, :], z[c][:, 0, :, :], ACT.Copy, scale=-1.0)
+            else:
+                nc.vector.tensor_scalar(out=z[c][:, 1, :, :], in0=z[c][:, 0, :, :], scalar1=-1.0, scalar2=None, op0=ALU.mult)
+
+        def score(c):
+            cols = slice(c * CHUNK, (c + 1) * CHUNK)
             z_c = keep.tile([P, 2 * CHUNK], U32, name="z_c%d" % c, align_bytes=64)
             z_s = keep.tile([P, 2 * CHUNK], U8, name="z_s%d" % c, align_bytes=64)
-
-            def quantise(s0, s1):
-                zc = slice(s0 * CHUNK, s1 * CHUNK)
-                nc.vector.quantize_mx(out=z_c[:, zc].bitcast(FP8X4), scales=z_s[:, zc], in_=z[:, s0:s1, :, :].rearrange("p s n t -> p (s n t)"))
-
-            if last:
-                quantise(0, 1)
-            nc.vector.tensor_scalar(out=z[:, 1, :, :], in0=z[:, 0, :, :], scalar1=-1.0, scalar2=None, op0=ALU.mult)
-            if last:
-                quantise(1, 2)
-            else:
-                quantise(0, 2)
-
-            groups = [(0, 2), (2, 4)] if last else [(0, 4)]
-            banks = []
+            nc.vector.quantize_mx(out=z_c[:].bitcast(FP8X4), scales=z_s[:], in_=z[c][:].rearrange("p s n t -> p (s n t)"))
+            groups = [(0, 2), (2, 4)] if c >= 3 else [(0, 4)]
             for g, (v0, v1) in enumerate(groups):
-                tag = "d%d" % c if g == 0 else "h0"
-                banks.append(psum.tile([P, v1 - v0, CHUNK], F32, name="d%d_%d" % (c, g), tag=tag))
-            for s, (xw, xs) in enumerate(((xa_w, xa_s), (xb_w, xb_s))):
-                zc = slice(s * CHUNK, (s + 1) * CHUNK)
-                for d, (v0, v1) in zip(banks, groups):
-                    for v in range(v0, v1):
-                        rows = slice(v * P, (v + 1) * P)
+                d = psum.tile([P, v1 - v0, CHUNK], F32, name="d%d_%d" % (c, g), tag="d%d" % c if g == 0 else "h%d" % c)
+                for v in range(v0, v1):
+                    rows = slice(v * P, (v + 1) * P)
+                    for s, (xw, xs) in enumerate(((xa_w, xa_s), (xb_w, xb_s))):
+                        zc = slice(s * CHUNK, (s + 1) * CHUNK)
                         nc.tensor.matmul_mx(
                             out=d[:, v - v0, :],
                             lhsT=xw[:, rows].bitcast(FP8X4),
                             lhsT_scale=xs[:, rows],
                             rhs=z_c[:, zc].bitcast(FP8X4),
                             rhs_scale=z_s[:, zc],
-                            start=(s == 0 and v == v0),
-                            stop=(s == 1 and v == v1 - 1),
+                            start=(s == 0),
+                            stop=(s == 1),
                         )
-            for g, (d, (v0, v1)) in enumerate(zip(banks, groups)):
                 res = keep.tile([P, v1 - v0, CHUNK], F32, name="res%d_%d" % (c, g))
                 nc.scalar.activation(res[:], d[:], ACT.Sigmoid, scale=0.0625)
                 nc.sync.dma_start(out_v[:, v0:v1, cols], res[:])
+
+        weigh(0)
+        negate(0)
+        weigh(1)
+        negate(1)
+        score(0)
+        weigh(2)
+        negate(2)
+        score(1)
+        weigh(3)
+        score(2)
+        negate(3)
+        score(3)

from contextlib import ExitStack

import concourse.mybir as mybir

K, T, S, V, H = 512, 2048, 512, 512, 512
FLOPS = 2 * K * H * S + 2 * 2 * H * V * S

F32 = mybir.dt.float32
BF16 = mybir.dt.bfloat16
I32 = mybir.dt.int32
U32 = mybir.dt.uint32
U16 = mybir.dt.uint16
U8 = mybir.dt.uint8
FP8X4 = mybir.dt.float8_e4m3fn_x4
ALU = mybir.AluOpType
ACT = mybir.ActivationFunctionType

P = 128
PACK = 4
CHUNK = 128
W_SPLIT = (0, 256, 512)


def tile_picked_candtwo_sigmoid_p_kernel(tc, x_words, x_scales, w1, gs, offs, ca, cb, out):
    nc = tc.nc
    with ExitStack() as ctx:
        keep = ctx.enter_context(tc.tile_pool(name="keep", bufs=1))
        shared = ctx.enter_context(tc.tile_pool(name="shared", bufs=1))
        psum = ctx.enter_context(tc.psum_pool(name="psum", bufs=1))

        offs_t = keep.tile([P, S // 16], U16, name="offs_t")
        ca_t = keep.tile([P, V // 16], U16, name="ca_t")
        cb_t = keep.tile([P, V // 16], U16, name="cb_t")
        words = keep.tile([P, T], U32, name="words", align_bytes=64)
        scales = shared.tile([P, T], U8, name="scales", align_bytes=64, offset=1024)
        gs_t = keep.tile([P, PACK], F32, name="gs_t")

        nc.vector.memset(scales[:].bitcast(I32), 0)
        nc.sync.dma_start(offs_t[:], offs)
        nc.sync.dma_start(ca_t[:], ca)
        nc.sync.dma_start(cb_t[:], cb)
        for q in range(4):
            queue = nc.sync if q < 2 else nc.scalar
            queue.dma_start(scales[32 * q : 32 * q + 4, :].bitcast(I32), x_scales[0, 4 * q : 4 * q + 4, :].bitcast(I32))
        warm = keep.tile([P, 2], F32, name="warm")
        nc.vector.memset(warm[:, 0:1], 0.0)
        nc.scalar.activation(warm[:, 1:2], warm[:, 0:1], ACT.Sigmoid, scale=0.0625)
        nc.sync.dma_start(words[:].bitcast(I32), x_words[0].rearrange("p n t -> p (n t)").bitcast(I32))
        w_rows = w1.rearrange("(p j) c -> p j c", j=PACK)
        w_pieces = list(zip(W_SPLIT[:-1], W_SPLIT[1:]))
        w_raw = []
        for lo, hi in w_pieces:
            raw = keep.tile([P, PACK, hi - lo], F32, name="w_raw%d" % lo)
            nc.sync.dma_start(raw[:], w_rows[:, :, lo:hi])
            w_raw.append(raw)
        nc.sync.dma_start(gs_t[:], gs.rearrange("(p t) o -> p (t o)", t=PACK))

        def gather(name, table, dtype, lst, offset=None):
            if offset is None:
                g = keep.tile([P, S], dtype, name=name, align_bytes=64)
            else:
                g = shared.tile([P, S], dtype, name=name, align_bytes=64, offset=offset)
            nc.vector.tensor_copy(g[:], table[:].indirect(lst[:]))
            return g

        xs_s = gather("xs_s", scales, U8, offs_t)
        xa_s = gather("xa_s", scales, U8, ca_t)
        xb_s = gather("xb_s", scales, U8, cb_t)
        xs_w = gather("xs_w", words, U32, offs_t, offset=0)
        xa_w = gather("xa_w", words, U32, ca_t, offset=2048)

        w_bf = shared.tile([P, PACK, P, PACK], BF16, name="w_bf", align_bytes=64, offset=4096)
        for raw, (lo, hi) in zip(w_raw, w_pieces):
            nc.scalar.copy(
                w_bf[:, :, lo // PACK : hi // PACK, :].rearrange("p t m j -> p m t j"),
                raw[:].rearrange("p j (m t) -> p m t j", t=PACK),
            )
        w_c = keep.tile([P, H], U32, name="w_c", align_bytes=64)
        w_s = keep.tile([P, H], U8, name="w_s", align_bytes=64)
        nc.vector.quantize_mx(out=w_c[:].bitcast(FP8X4), scales=w_s[:], in_=w_bf[:].rearrange("p t m j -> p (t m j)"))

        xb_w = gather("xb_w", words, U32, cb_t, offset=4096)

        n_chunks = S // CHUNK
        h_banks = []
        for c in range(n_chunks):
            cols = slice(c * CHUNK, (c + 1) * CHUNK)
            h = psum.tile([P, PACK, CHUNK], F32, name="h%d" % c)
            for t in range(PACK):
                ch = slice(t * P, (t + 1) * P)
                nc.tensor.matmul_mx(
                    out=h[:, t, :],
                    lhsT=w_c[:, ch].bitcast(FP8X4),
                    lhsT_scale=w_s[:, ch],
                    rhs=xs_w[:, cols].bitcast(FP8X4),
                    rhs_scale=xs_s[:, cols],
                    start=True,
                    stop=True,
                )
            h_banks.append(h)

        out_v = out.rearrange("(v p) s -> p v s", p=P)
        n_blocks = V // P
        z = [keep.tile([P, 2, CHUNK, PACK], BF16, name="z%d" % c, align_bytes=64) for c in range(n_chunks)]

        def weigh(c):
            nc.vector.scalar_tensor_tensor(
                out=z[c][:, 0, :, :],
                in0=h_banks[c][:].rearrange("p t n -> p n t"),
                scalar=0.0,
                in1=gs_t[:].unsqueeze(1).to_broadcast([P, CHUNK, PACK]),
                op0=ALU.max,
                op1=ALU.mult,
            )

        def negate(c):
            if c in (0, 1, 2):
                nc.scalar.activation(z[c][:, 1, :, :], z[c][:, 0, :, :], ACT.Copy, scale=-1.0)
            else:
                nc.vector.tensor_scalar(out=z[c][:, 1, :, :], in0=z[c][:, 0, :, :], scalar1=-1.0, scalar2=None, op0=ALU.mult)

        def score(c):
            cols = slice(c * CHUNK, (c + 1) * CHUNK)
            z_c = keep.tile([P, 2 * CHUNK], U32, name="z_c%d" % c, align_bytes=64)
            z_s = keep.tile([P, 2 * CHUNK], U8, name="z_s%d" % c, align_bytes=64)
            nc.vector.quantize_mx(out=z_c[:].bitcast(FP8X4), scales=z_s[:], in_=z[c][:].rearrange("p s n t -> p (s n t)"))
            groups = [(0, 2), (2, 4)] if c >= 3 else [(0, 4)]
            for g, (v0, v1) in enumerate(groups):
                d = psum.tile([P, v1 - v0, CHUNK], F32, name="d%d_%d" % (c, g), tag="d%d" % c if g == 0 else "h%d" % c)
                for v in range(v0, v1):
                    rows = slice(v * P, (v + 1) * P)
                    for s, (xw, xs) in enumerate(((xa_w, xa_s), (xb_w, xb_s))):
                        zc = slice(s * CHUNK, (s + 1) * CHUNK)
                        nc.tensor.matmul_mx(
                            out=d[:, v - v0, :],
                            lhsT=xw[:, rows].bitcast(FP8X4),
                            lhsT_scale=xs[:, rows],
                            rhs=z_c[:, zc].bitcast(FP8X4),
                            rhs_scale=z_s[:, zc],
                            start=(s == 0),
                            stop=(s == 1),
                        )
                res = keep.tile([P, v1 - v0, CHUNK], F32, name="res%d_%d" % (c, g))
                nc.scalar.activation(res[:], d[:], ACT.Sigmoid, scale=0.0625)
                nc.sync.dma_start(out_v[:, v0:v1, cols], res[:])

        weigh(0)
        negate(0)
        weigh(1)
        negate(1)
        score(0)
        weigh(2)
        negate(2)
        score(1)
        weigh(3)
        score(2)
        negate(3)
        score(3)
